import numpy as np
import ml_dtypes


def mxq(x, axis, fmt="e4m3"):
    dtype, down = {"e4m3": (ml_dtypes.float8_e4m3fn, 7), "e5m2": (ml_dtypes.float8_e5m2, 14)}[fmt]
    v = np.moveaxis(np.asarray(x, np.float32).astype(ml_dtypes.bfloat16).astype(np.float64), axis, -1)
    blocks = v.reshape(v.shape[:-1] + (-1, 32))
    amax = np.abs(blocks).max(-1, keepdims=True)
    byte = np.maximum(np.where(amax > 0, np.frexp(amax)[1] - 1 + 127, 0) - down, 1)
    scale = np.exp2(byte - 127.0)
    codes = (blocks / scale).astype(np.float32).astype(dtype).astype(np.float64)
    return np.moveaxis((codes * scale).reshape(v.shape), -1, axis)


WIDE = False


def mx_kscale(k):
    if not WIDE:
        return np.ones(k)
    levels = np.array([18, -18])
    if k % 512:
        return np.exp2(np.random.permutation(np.resize(levels, k // 32))).repeat(32)
    a = np.empty((k // 512, 16))
    for p in range(k // 512):
        a[p, :8] = np.random.permutation(np.resize(levels, 8))
        for g in range(8):
            far = levels[np.abs(levels - a[p, g]) >= 10]
            a[p, g + 8] = far[np.random.randint(len(far))]
    return np.exp2(a.ravel()).repeat(32)


def f64(x):
    return np.asarray(x).astype(np.float64)


def striped(idx):
    return np.tile(np.asarray(idx).reshape(-1, 16).T, (8, 1)).astype(np.uint16)


def unstriped(offs):
    return offs[:16].T.reshape(-1).astype(np.int64)

def planes(y):
    n, m = y.shape
    v = y.astype(np.float32).astype(ml_dtypes.bfloat16).astype(np.float64).reshape(n // 32, 32, m)
    top = np.abs(v).max(1)
    byte = np.clip(np.where(top > 0, np.frexp(top)[1] - 1 + 127 - 7, 1), 1, 254)
    codes = (v * np.exp2(127.0 - byte)[:, None, :]).reshape(n, m).astype(np.float32).astype(ml_dtypes.float8_e4m3fn).view(np.uint8)
    words = codes.reshape(n // 512, 128, 4, m).transpose(0, 1, 3, 2)
    return np.ascontiguousarray(words), np.ascontiguousarray(byte.astype(np.uint8).reshape(n // 512, 16, m))


def setup_inputs():
    n = np.random.standard_normal
    uni = np.random.uniform
    idx = np.random.permutation(1024)[:512]
    jdx = np.random.permutation(1024)[:512]
    f_f = mx_kscale(512)
    f_r = mx_kscale(512)
    return {
        "V": (n((512, 512)) / np.sqrt(512) * f_f[:, None]).astype(np.float32),
        "dz": (n((512, 512)) / f_f[:, None]).astype(np.float32),
        "xT": (n((512, 512)) * f_r[None, :]).astype(np.float32),
        "G": (n((512, 512)) / np.sqrt(512) / f_r[:, None]).astype(np.float32),
        "offs": striped(idx),
        "joffs": striped(jdx),
    }


def reference(V, dz, xT, G, offs, joffs):
    idx = unstriped(offs)
    jdx = unstriped(joffs)
    da = mxq(f64(V), 0, "e4m3").T @ mxq(f64(dz), 0, "e5m2")
    db = mxq(f64(xT), 1, "e4m3") @ mxq(f64(G), 0, "e5m2")
    pa = np.zeros((512, 1024))
    pa[:, jdx] = da
    pb = np.zeros((512, 1024))
    pb[:, idx] = db
    out_0 = pa + pb
    return (out_0,) + planes(out_0)

@@ -1,0 +1,212 @@
+from contextlib import ExitStack
+
+import concourse.mybir as mybir
+from concourse.masks import make_identity
+
+F32 = mybir.dt.float32
+BF16 = mybir.dt.bfloat16
+I32 = mybir.dt.int32
+U32 = mybir.dt.uint32
+U16 = mybir.dt.uint16
+U8 = mybir.dt.uint8
+E4M3 = mybir.dt.float8_e4m3fn_x4
+E5M2 = mybir.dt.float8_e5m2_x4
+ADD = mybir.AluOpType.add
+
+P = 128
+LANES = 4
+K = P * LANES
+SLOTS = 512
+TOKENS = 1024
+G_CHUNKS = (256, 128, 128)
+
+FLOPS = 2 * 2 * K * K * SLOTS
+
+
+def tile_attend_gtied_pl_kernel(tc, V, dz, xT, G, offs, joffs, out_0, out_1, out_2):
+    nc = tc.nc
+    with ExitStack() as ctx:
+        sb = ctx.enter_context(tc.tile_pool(name="sb", bufs=1))
+        ps = ctx.enter_context(tc.psum_pool(name="ps", bufs=1))
+
+        def tile(name, shape, dtype, tag=None):
+            return sb.tile(shape, dtype, name=name, tag=tag or name, align_bytes=64)
+
+        x_rows = xT.rearrange("(m t) r -> m t r", t=LANES)
+        x_raw = [tile("x_raw%d" % t, [P, K], F32) for t in range(LANES)]
+        nc.sync.dma_start(out=x_raw[0][:], in_=x_rows[:, 0, :])
+        g_rows = G.rearrange("(p j) i -> p j i", j=LANES)
+        g_raw = []
+        start = 0
+        for c, width in enumerate(G_CHUNKS):
+            raw = tile("g_raw%d" % c, [P, LANES, width], F32)
+            nc.sync.dma_start(out=raw[:], in_=g_rows[:, :, start : start + width])
+            g_raw.append((raw, start, width))
+            start = start + width
+        last = len(G_CHUNKS) - 1
+        idx = sb.tile([P, SLOTS // 16], U16, name="idx")
+        nc.sync.dma_start(idx[:], offs)
+        for t in range(1, LANES):
+            nc.sync.dma_start(out=x_raw[t][:], in_=x_rows[:, t, :])
+        dz_raw = tile("dz_raw", [P, LANES, SLOTS], F32)
+        nc.sync.dma_start(out=dz_raw[:], in_=dz.rearrange("(p j) s -> p j s", j=LANES))
+        v_raw = tile("v_raw", [P, LANES, K], F32)
+        nc.sync.dma_start(out=v_raw[:], in_=V.rearrange("(p j) d -> p j d", j=LANES))
+        jdx = sb.tile([P, SLOTS // 16], U16, name="jdx")
+        nc.sync.dma_start(jdx[:], joffs)
+
+        ident = tile("ident", [P, P], F32)
+        make_identity(nc, ident[:])
+
+        pb = [tile("pb%d" % t, [P, TOKENS], F32) for t in range(LANES)]
+        pa = [tile("pa%d" % t, [P, TOKENS], F32) for t in range(2)]
+        for window in pb + pa:
+            nc.vector.memset(window[:], 0.0)
+
+        def interleave(copy, grouped, raw):
+            copy(
+                out=grouped.rearrange("p (c i) j -> p c j i", i=4),
+                in_=raw.rearrange("p j (c i) -> p c j i", i=4),
+            )
+
+        def quantise(name, grouped, fmt):
+            width = grouped.shape[1] // LANES
+            codes = tile(name + "_codes", [P, width], U32)
+            scales = tile(name + "_scales", [P, width], U8)
+            nc.vector.quantize_mx(out=codes[:].bitcast(fmt), scales=scales[:], in_=grouped)
+            return codes[:], scales[:]
+
+        def x_by_pairs(t, cast, pairs_tag, bank_tag):
+            pairs = tile("x_pairs%d" % t, [P, K], BF16, tag=pairs_tag)
+            cast(
+                out=pairs[:].rearrange("m (u p e) -> m u p e", u=2, e=2),
+                in_=x_raw[t][:].rearrange("m (p u e) -> m u p e", u=2, e=2),
+            )
+            words = pairs[:].bitcast(F32)
+            turned = ps.tile([P, 2, P], F32, name="turned%d" % t, tag=bank_tag)
+            for u in range(2):
+                nc.tensor.transpose(turned[:, u, :], words[:, u * P : (u + 1) * P], ident[:])
+            grouped = tile("x_grouped%d" % t, [P, K], BF16)
+            nc.scalar.copy(
+                out=grouped[:].bitcast(F32).rearrange("p (m u) -> p m u", u=2),
+                in_=turned[:].rearrange("p u m -> p m u"),
+            )
+            return quantise("x%d" % t, grouped[:], E4M3)
+
+        def product(name, stationary, moving, bank_tag):
+            bank = ps.tile([P, SLOTS], F32, name="bank_" + name, tag=bank_tag)
+            nc.tensor.matmul_mx(
+                out=bank[:],
+                lhsT=stationary[0].bitcast(E4M3),
+                lhsT_scale=stationary[1],
+                rhs=moving[0].bitcast(E5M2),
+                rhs_scale=moving[1],
+                start=True,
+                stop=True,
+            )
+            return bank
+
+        def scatter(name, window, offsets, bank, first, count, tag=None):
+            staged = tile(name, [P, count], F32, tag=tag)
+            nc.scalar.copy(out=staged[:], in_=bank[:, first : first + count])
+            entries = offsets[:, first // 16 : (first + count) // 16]
+            nc.vector.tensor_copy(window[:].indirect(entries), staged[:])
+            return staged
+
+        x0 = x_by_pairs(0, nc.scalar.copy, None, "turned")
+        g_codes = tile("g_codes", [P, SLOTS], U32)
+        g_scales = tile("g_scales", [P, SLOTS], U8)
+        for c, (raw, start, width) in enumerate(g_raw):
+            grouped = tile("g_grouped%d" % c, [P, width, LANES], BF16)
+            interleave(nc.scalar.copy if c == 0 else nc.vector.tensor_copy, grouped[:], raw[:])
+            nc.vector.quantize_mx(
+                out=g_codes[:, start : start + width].bitcast(E5M2),
+                scales=g_scales[:, start : start + width],
+                in_=grouped[:].rearrange("p c j -> p (c j)"),
+            )
+        g_quant = (g_codes[:], g_scales[:])
+
+        half_slots = SLOTS // 2
+        dz_codes = tile("dz_codes", [P, SLOTS], U32)
+        dz_scales = tile("dz_scales", [P, SLOTS], U8)
+        x_quant = x0
+        freed = "g_grouped%d" % last
+        for t in range(LANES - 1):
+            db = product("db%d" % t, x_quant, g_quant, "bank_db%d" % (t % 2))
+            staged = scatter("db%da" % t, pb[t], idx, db, 0, half_slots)
+            x_quant = x_by_pairs(t + 1, nc.scalar.copy, freed, "turned")
+            scatter("db%db" % t, pb[t], idx, db, half_slots, half_slots, tag=freed)
+            freed = "x_grouped%d" % (t + 1)
+            if t > 0:
+                cols = slice((t - 1) * half_slots, t * half_slots)
+                grouped = tile("dz_grouped%d" % t, [P, half_slots, LANES], BF16, tag="x%d_codes" % t)
+                interleave(nc.scalar.copy, grouped[:], dz_raw[:, :, cols])
+                nc.vector.quantize_mx(
+                    out=dz_codes[:, cols].bitcast(E5M2),
+                    scales=dz_scales[:, cols],
+                    in_=grouped[:].rearrange("p c j -> p (c j)"),
+                )
+        dz_quant = (dz_codes[:], dz_scales[:])
+        v_grouped = tile("v_grouped", [P, LANES * K], BF16, tag="dz_raw")
+        nc.scalar.copy(
+            out=v_grouped[:].rearrange("p (t m j) -> p m t j", t=LANES, j=LANES),
+            in_=v_raw[:].rearrange("p j (m t) -> p m t j", t=LANES),
+        )
+        v_codes, v_scales = quantise("v", v_grouped[:], E4M3)
+
+        db = product("db3", x_quant, g_quant, "bank_db1")
+        scatter("db3", pb[3], idx, db, 0, SLOTS, tag="v_raw")
+
+        out_rows = out_0.rearrange("(p t) c -> p t c", t=LANES)
+        sums = [tile("sums%d" % h, [P, 2 * TOKENS], F32) for h in range(2)]
+        rounded = tile("rounded", [P, LANES * TOKENS], BF16)
+        rounded_cols = rounded[:].rearrange("p (c j) -> p c j", j=LANES)
+
+        def round_pair(copy, h, cols):
+            copy(
+                out=rounded_cols[:, cols, 2 * h : 2 * h + 2],
+                in_=sums[h][:].rearrange("p (e c) -> p c e", e=2)[:, cols, :],
+            )
+
+        for t in range(LANES):
+            cols = slice(t * P, (t + 1) * P)
+            da = product("da%d" % t, (v_codes[:, cols], v_scales[:, cols]), dz_quant, "bank_da%d" % t)
+            scatter("da%d" % t, pa[t % 2], jdx, da, 0, SLOTS)
+            total = sums[t // 2][:, (t % 2) * TOKENS : (t % 2 + 1) * TOKENS]
+            if t < LANES - 1:
+                nc.vector.tensor_tensor(total, pa[t % 2][:], pb[t][:], ADD)
+                nc.sync.dma_start(out=out_rows[:, t, :], in_=total)
+            if t == 1:
+                round_pair(nc.scalar.copy, 0, slice(0, TOKENS))
+
+        quarter = TOKENS // 4
+        half = TOKENS // 2
+        for q in range(4):
+            cols = slice(q * quarter, (q + 1) * quarter)
+            nc.vector.tensor_tensor(total[:, cols], pa[1][:, cols], pb[3][:, cols], ADD)
+            if q < 2:
+                round_pair(nc.scalar.copy, 1, cols)
+            if q % 2 == 1:
+                cols = slice((q // 2) * half, (q // 2 + 1) * half)
+                nc.sync.dma_start(out=out_rows[:, 3, cols], in_=total[:, cols])
+        for q in range(2, 4):
+            round_pair(nc.vector.tensor_copy, 1, slice(q * quarter, (q + 1) * quarter))
+
+        words = tile("words", [P, TOKENS], U32)
+        scales = tile("scales", [P, TOKENS], U8)
+        words_out = out_1.rearrange("a p c j -> p (a c j)").bitcast(I32)
+        for h in range(2):
+            cols = slice(h * half, (h + 1) * half)
+            nc.vector.quantize_mx(
+                out=words[:, cols].bitcast(E4M3),
+                scales=scales[:, cols],
+                in_=rounded[:, h * half * LANES : (h + 1) * half * LANES],
+            )
+            nc.sync.dma_start(out=words_out[:, cols], in_=words[:, cols].bitcast(I32))
+        scales_out = out_2.rearrange("a b c -> (a b) c").bitcast(I32)
+        for quadrant in range(4):
+            queue = nc.scalar if quadrant % 2 == 0 else nc.sync
+            queue.dma_start(
+                out=scales_out[4 * quadrant : 4 * quadrant + 4, :],
+                in_=scales[32 * quadrant : 32 * quadrant + 4, :].bitcast(I32),
+            )

@@ -58,10 +58,12 @@ def tile_attend_gtied_pl_kernel(tc, V, dz, xT, G, offs, joffs, out_0, out_1, out
         ident = tile("ident", [P, P], F32)
         make_identity(nc, ident[:])
 
-        pb = [tile("pb%d" % t, [P, TOKENS], F32) for t in range(LANES)]
-        pa = [tile("pa%d" % t, [P, TOKENS], F32) for t in range(2)]
-        for window in pb + pa:
-            nc.vector.memset(window[:], 0.0)
+        def window(name, engine, tag=None):
+            cleared = tile(name, [P, TOKENS], F32, tag=tag)
+            engine.memset(cleared[:].bitcast(I32), 0)
+            return cleared
+
+        pb = [window("pb0", nc.vector), window("pb1", nc.gpsimd), window("pb2", nc.vector)]
 
         def interleave(copy, grouped, raw):
             copy(
@@ -113,7 +115,7 @@ def tile_attend_gtied_pl_kernel(tc, V, dz, xT, G, offs, joffs, out_0, out_1, out
             nc.vector.tensor_copy(window[:].indirect(entries), staged[:])
             return staged
 
-        x0 = x_by_pairs(0, nc.scalar.copy, None, "turned")
+        x0 = x_by_pairs(0, nc.vector.tensor_copy, None, "turned")
         g_codes = tile("g_codes", [P, SLOTS], U32)
         g_scales = tile("g_scales", [P, SLOTS], U8)
         for c, (raw, start, width) in enumerate(g_raw):
@@ -155,6 +157,8 @@ def tile_attend_gtied_pl_kernel(tc, V, dz, xT, G, offs, joffs, out_0, out_1, out
         v_codes, v_scales = quantise("v", v_grouped[:], E4M3)
 
         db = product("db3", x_quant, g_quant, "bank_db1")
+        pb.append(window("pb3", nc.gpsimd, tag="x1_scales"))
+        pa = [window("pa%d" % t, nc.gpsimd, tag="x%d_scales" % (t + 2)) for t in range(2)]
         scatter("db3", pb[3], idx, db, 0, SLOTS, tag="v_raw")
 
         out_rows = out_0.rearrange("(p t) c -> p t c", t=LANES)
@@ -174,7 +178,7 @@ def tile_attend_gtied_pl_kernel(tc, V, dz, xT, G, offs, joffs, out_0, out_1, out
             scatter("da%d" % t, pa[t % 2], jdx, da, 0, SLOTS)
             total = sums[t // 2][:, (t % 2) * TOKENS : (t % 2 + 1) * TOKENS]
             if t < LANES - 1:
-                nc.vector.tensor_tensor(total, pa[t % 2][:], pb[t][:], ADD)
+                nc.gpsimd.tensor_tensor(total, pa[t % 2][:], pb[t][:], ADD)
                 nc.sync.dma_start(out=out_rows[:, t, :], in_=total)
             if t == 1:
                 round_pair(nc.scalar.copy, 0, slice(0, TOKENS))

@@ -17,8 +17,8 @@ P = 128
 LANES = 4
 K = P * LANES
 SLOTS = 512
+HALF = SLOTS // 2
 TOKENS = 1024
-G_CHUNKS = (256, 128, 128)
 
 FLOPS = 2 * 2 * K * K * SLOTS
 
@@ -36,22 +36,18 @@ def tile_attend_gtied_pl_kernel(tc, V, dz, xT, G, offs, joffs, out_0, out_1, out
         x_raw = [tile("x_raw%d" % t, [P, K], F32) for t in range(LANES)]
         nc.sync.dma_start(out=x_raw[0][:], in_=x_rows[:, 0, :])
         g_rows = G.rearrange("(p j) i -> p j i", j=LANES)
-        g_raw = []
-        start = 0
-        for c, width in enumerate(G_CHUNKS):
-            raw = tile("g_raw%d" % c, [P, LANES, width], F32)
-            nc.sync.dma_start(out=raw[:], in_=g_rows[:, :, start : start + width])
-            g_raw.append((raw, start, width))
-            start = start + width
-        last = len(G_CHUNKS) - 1
+        g_raw = [tile("g_raw%d" % h, [P, LANES, HALF], F32) for h in range(2)]
+        for h in range(2):
+            nc.sync.dma_start(out=g_raw[h][:], in_=g_rows[:, :, h * HALF : (h + 1) * HALF])
         idx = sb.tile([P, SLOTS // 16], U16, name="idx")
         nc.sync.dma_start(idx[:], offs)
-        for t in range(1, LANES):
+        for t in (1, 2):
             nc.sync.dma_start(out=x_raw[t][:], in_=x_rows[:, t, :])
-        dz_raw = tile("dz_raw", [P, LANES, SLOTS], F32)
-        nc.sync.dma_start(out=dz_raw[:], in_=dz.rearrange("(p j) s -> p j s", j=LANES))
         v_raw = tile("v_raw", [P, LANES, K], F32)
         nc.sync.dma_start(out=v_raw[:], in_=V.rearrange("(p j) d -> p j d", j=LANES))
+        nc.sync.dma_start(out=x_raw[3][:], in_=x_rows[:, 3, :])
+        dz_raw = tile("dz_raw", [P, LANES, SLOTS], F32)
+        nc.sync.dma_start(out=dz_raw[:], in_=dz.rearrange("(p j) s -> p j s", j=LANES))
         jdx = sb.tile([P, SLOTS // 16], U16, name="jdx")
         nc.sync.dma_start(jdx[:], joffs)
 
@@ -63,11 +59,15 @@ def tile_attend_gtied_pl_kernel(tc, V, dz, xT, G, offs, joffs, out_0, out_1, out
             engine.memset(cleared[:].bitcast(I32), 0)
             return cleared
 
-        pb = [window("pb0", nc.vector), window("pb1", nc.gpsimd), window("pb2", nc.vector)]
+        g_codes = tile("g_codes", [P, HALF + SLOTS], U32)
+        g_scales = tile("g_scales", [P, HALF + SLOTS], U8)
+        nc.vector.memset(g_codes[:, 0:HALF], 0)
+        nc.vector.memset(g_scales[:, 0:HALF].bitcast(U32), 0)
+        pb = [window("pb0", nc.vector), window("pb1", nc.vector)]
 
         def interleave(copy, grouped, raw):
             copy(
-                out=grouped.rearrange("p (c i) j -> p c j i", i=4),
+                out=grouped.rearrange("p (c i j) -> p c j i", i=4, j=LANES),
                 in_=raw.rearrange("p j (c i) -> p c j i", i=4),
             )
 
@@ -78,22 +78,21 @@ def tile_attend_gtied_pl_kernel(tc, V, dz, xT, G, offs, joffs, out_0, out_1, out
             nc.vector.quantize_mx(out=codes[:].bitcast(fmt), scales=scales[:], in_=grouped)
             return codes[:], scales[:]
 
-        def x_by_pairs(t, cast, pairs_tag, bank_tag):
+        def quantise_x(t, cast, pairs_tag, grouped):
             pairs = tile("x_pairs%d" % t, [P, K], BF16, tag=pairs_tag)
             cast(
                 out=pairs[:].rearrange("m (u p e) -> m u p e", u=2, e=2),
                 in_=x_raw[t][:].rearrange("m (p u e) -> m u p e", u=2, e=2),
             )
             words = pairs[:].bitcast(F32)
-            turned = ps.tile([P, 2, P], F32, name="turned%d" % t, tag=bank_tag)
+            turned = ps.tile([P, 2, P], F32, name="turned%d" % t, tag="turned")
             for u in range(2):
                 nc.tensor.transpose(turned[:, u, :], words[:, u * P : (u + 1) * P], ident[:])
-            grouped = tile("x_grouped%d" % t, [P, K], BF16)
             nc.scalar.copy(
-                out=grouped[:].bitcast(F32).rearrange("p (m u) -> p m u", u=2),
+                out=grouped.bitcast(F32).rearrange("p (m u) -> p m u", u=2),
                 in_=turned[:].rearrange("p u m -> p m u"),
             )
-            return quantise("x%d" % t, grouped[:], E4M3)
+            return quantise("x%d" % t, grouped, E4M3)
 
         def product(name, stationary, moving, bank_tag):
             bank = ps.tile([P, SLOTS], F32, name="bank_" + name, tag=bank_tag)
@@ -108,58 +107,60 @@ def tile_attend_gtied_pl_kernel(tc, V, dz, xT, G, offs, joffs, out_0, out_1, out
             )
             return bank
 
-        def scatter(name, window, offsets, bank, first, count, tag=None):
+        def scatter(name, target, offsets, first, results, tag=None):
+            count = results.shape[1]
             staged = tile(name, [P, count], F32, tag=tag)
-            nc.scalar.copy(out=staged[:], in_=bank[:, first : first + count])
+            nc.scalar.copy(out=staged[:], in_=results)
             entries = offsets[:, first // 16 : (first + count) // 16]
-            nc.vector.tensor_copy(window[:].indirect(entries), staged[:])
+            nc.vector.tensor_copy(target[:].indirect(entries), staged[:])
             return staged
 
-        x0 = x_by_pairs(0, nc.vector.tensor_copy, None, "turned")
-        g_codes = tile("g_codes", [P, SLOTS], U32)
-        g_scales = tile("g_scales", [P, SLOTS], U8)
-        for c, (raw, start, width) in enumerate(g_raw):
-            grouped = tile("g_grouped%d" % c, [P, width, LANES], BF16)
-            interleave(nc.scalar.copy if c == 0 else nc.vector.tensor_copy, grouped[:], raw[:])
-            nc.vector.quantize_mx(
-                out=g_codes[:, start : start + width].bitcast(E5M2),
-                scales=g_scales[:, start : start + width],
-                in_=grouped[:].rearrange("p c j -> p (c j)"),
-            )
-        g_quant = (g_codes[:], g_scales[:])
+        head = tile("head", [P, LANES * HALF + K], BF16)
+        x_quant = quantise_x(0, nc.vector.tensor_copy, None, head[:, LANES * HALF :])
 
-        half_slots = SLOTS // 2
-        dz_codes = tile("dz_codes", [P, SLOTS], U32)
-        dz_scales = tile("dz_scales", [P, SLOTS], U8)
-        x_quant = x0
-        freed = "g_grouped%d" % last
+        def quantise_g(h, grouped):
+            interleave(nc.vector.tensor_copy, grouped, g_raw[h][:])
+            cols = slice((h + 1) * HALF, (h + 2) * HALF)
+            nc.vector.quantize_mx(out=g_codes[:, cols].bitcast(E5M2), scales=g_scales[:, cols], in_=grouped)
+
+        quantise_g(0, head[:, : LANES * HALF])
+        early = product("early", x_quant, (g_codes[:, :SLOTS], g_scales[:, :SLOTS]), "bank_early")
+        quantise_g(1, head[:, K:])
+        g_quant = (g_codes[:, HALF:], g_scales[:, HALF:])
+
+        def quantise_v(h, tag):
+            grouped = tile("v_grouped%d" % h, [P, 2 * K], BF16, tag=tag)
+            nc.scalar.copy(
+                out=grouped[:].rearrange("p (t m j) -> p m t j", t=2, j=LANES),
+                in_=v_raw[:].rearrange("p j (m t) -> p m t j", t=LANES)[:, :, 2 * h : 2 * h + 2, :],
+            )
+            return quantise("v%d" % h, grouped[:], E4M3)
+
+        freed = "head"
         for t in range(LANES - 1):
             db = product("db%d" % t, x_quant, g_quant, "bank_db%d" % (t % 2))
-            staged = scatter("db%da" % t, pb[t], idx, db, 0, half_slots)
-            x_quant = x_by_pairs(t + 1, nc.scalar.copy, freed, "turned")
-            scatter("db%db" % t, pb[t], idx, db, half_slots, half_slots, tag=freed)
+            staged = scatter("db%da" % t, pb[t], idx, 0, early[:, HALF:] if t == 0 else db[:, :HALF])
+            grouped = tile("x_grouped%d" % (t + 1), [P, K], BF16)
+            x_quant = quantise_x(t + 1, nc.scalar.copy, freed, grouped[:])
+            scatter("db%db" % t, pb[t], idx, HALF, db[:, HALF:], tag=freed)
             freed = "x_grouped%d" % (t + 1)
-            if t > 0:
-                cols = slice((t - 1) * half_slots, t * half_slots)
-                grouped = tile("dz_grouped%d" % t, [P, half_slots, LANES], BF16, tag="x%d_codes" % t)
-                interleave(nc.scalar.copy, grouped[:], dz_raw[:, :, cols])
-                nc.vector.quantize_mx(
-                    out=dz_codes[:, cols].bitcast(E5M2),
-                    scales=dz_scales[:, cols],
-                    in_=grouped[:].rearrange("p c j -> p (c j)"),
-                )
-        dz_quant = (dz_codes[:], dz_scales[:])
-        v_grouped = tile("v_grouped", [P, LANES * K], BF16, tag="dz_raw")
-        nc.scalar.copy(
-            out=v_grouped[:].rearrange("p (t m j) -> p m t j", t=LANES, j=LANES),
-            in_=v_raw[:].rearrange("p j (m t) -> p m t j", t=LANES),
-        )
-        v_codes, v_scales = quantise("v", v_grouped[:], E4M3)
+            if t < 2:
+                pb.append(window("pb%d" % (t + 2), nc.gpsimd, tag="x%d_scales" % t))
+            if t == 1:
+                v_quant = [quantise_v(0, "x1_codes")]
 
+        dz_grouped = tile("dz_grouped", [P, LANES * SLOTS], BF16, tag="x2_codes")
+        for h in range(2):
+            interleave(
+                nc.scalar.copy,
+                dz_grouped[:, h * LANES * HALF : (h + 1) * LANES * HALF],
+                dz_raw[:, :, h * HALF : (h + 1) * HALF],
+            )
+        dz_quant = quantise("dz", dz_grouped[:], E5M2)
         db = product("db3", x_quant, g_quant, "bank_db1")
-        pb.append(window("pb3", nc.gpsimd, tag="x1_scales"))
-        pa = [window("pa%d" % t, nc.gpsimd, tag="x%d_scales" % (t + 2)) for t in range(2)]
-        scatter("db3", pb[3], idx, db, 0, SLOTS, tag="v_raw")
+        scatter("db3", pb[3], idx, 0, db[:], tag="dz_raw")
+        v_quant.append(quantise_v(1, "x3_codes"))
+        pa = [window("pa0", nc.gpsimd, tag="x3_scales"), window("pa1", nc.gpsimd, tag="x2_codes")]
 
         out_rows = out_0.rearrange("(p t) c -> p t c", t=LANES)
         sums = [tile("sums%d" % h, [P, 2 * TOKENS], F32) for h in range(2)]
@@ -173,9 +174,10 @@ def tile_attend_gtied_pl_kernel(tc, V, dz, xT, G, offs, joffs, out_0, out_1, out
             )
 
         for t in range(LANES):
-            cols = slice(t * P, (t + 1) * P)
+            cols = slice((t % 2) * P, (t % 2 + 1) * P)
+            v_codes, v_scales = v_quant[t // 2]
             da = product("da%d" % t, (v_codes[:, cols], v_scales[:, cols]), dz_quant, "bank_da%d" % t)
-            scatter("da%d" % t, pa[t % 2], jdx, da, 0, SLOTS)
+            scatter("da%d" % t, pa[t % 2], jdx, 0, da[:])
             total = sums[t // 2][:, (t % 2) * TOKENS : (t % 2 + 1) * TOKENS]
             if t < LANES - 1:
                 nc.gpsimd.tensor_tensor(total, pa[t % 2][:], pb[t][:], ADD)
@@ -199,12 +201,12 @@ def tile_attend_gtied_pl_kernel(tc, V, dz, xT, G, offs, joffs, out_0, out_1, out
         words = tile("words", [P, TOKENS], U32)
         scales = tile("scales", [P, TOKENS], U8)
         words_out = out_1.rearrange("a p c j -> p (a c j)").bitcast(I32)
-        for h in range(2):
-            cols = slice(h * half, (h + 1) * half)
+        for first, last in ((0, half), (half, half + quarter), (half + quarter, TOKENS)):
+            cols = slice(first, last)
             nc.vector.quantize_mx(
                 out=words[:, cols].bitcast(E4M3),
                 scales=scales[:, cols],
-                in_=rounded[:, h * half * LANES : (h + 1) * half * LANES],
+                in_=rounded[:, first * LANES : last * LANES],
             )
             nc.sync.dma_start(out=words_out[:, cols], in_=words[:, cols].bitcast(I32))
         scales_out = out_2.rearrange("a b c -> (a b) c").bitcast(I32)

@@ -18,6 +18,7 @@ LANES = 4
 K = P * LANES
 SLOTS = 512
 HALF = SLOTS // 2
+QUARTER = SLOTS // 4
 TOKENS = 1024
 
 FLOPS = 2 * 2 * K * K * SLOTS
@@ -36,9 +37,11 @@ def tile_attend_gtied_pl_kernel(tc, V, dz, xT, G, offs, joffs, out_0, out_1, out
         x_raw = [tile("x_raw%d" % t, [P, K], F32) for t in range(LANES)]
         nc.sync.dma_start(out=x_raw[0][:], in_=x_rows[:, 0, :])
         g_rows = G.rearrange("(p j) i -> p j i", j=LANES)
-        g_raw = [tile("g_raw%d" % h, [P, LANES, HALF], F32) for h in range(2)]
-        for h in range(2):
-            nc.sync.dma_start(out=g_raw[h][:], in_=g_rows[:, :, h * HALF : (h + 1) * HALF])
+        g_raw = []
+        for first, last in ((0, QUARTER), (QUARTER, HALF), (HALF, SLOTS)):
+            raw = tile("g_raw%d" % first, [P, LANES, last - first], F32)
+            nc.sync.dma_start(out=raw[:], in_=g_rows[:, :, first:last])
+            g_raw.append(raw)
         idx = sb.tile([P, SLOTS // 16], U16, name="idx")
         nc.sync.dma_start(idx[:], offs)
         for t in (1, 2):
@@ -63,7 +66,7 @@ def tile_attend_gtied_pl_kernel(tc, V, dz, xT, G, offs, joffs, out_0, out_1, out
         g_scales = tile("g_scales", [P, HALF + SLOTS], U8)
         nc.vector.memset(g_codes[:, 0:HALF], 0)
         nc.vector.memset(g_scales[:, 0:HALF].bitcast(U32), 0)
-        pb = [window("pb0", nc.vector), window("pb1", nc.vector)]
+        pb = [window("pb0", nc.vector), window("pb1", nc.gpsimd)]
 
         def interleave(copy, grouped, raw):
             copy(
@@ -115,17 +118,20 @@ def tile_attend_gtied_pl_kernel(tc, V, dz, xT, G, offs, joffs, out_0, out_1, out
             nc.vector.tensor_copy(target[:].indirect(entries), staged[:])
             return staged
 
-        head = tile("head", [P, LANES * HALF + K], BF16)
-        x_quant = quantise_x(0, nc.vector.tensor_copy, None, head[:, LANES * HALF :])
+        head = tile("head", [P, 7 * HALF], BF16)
+        x_quant = quantise_x(0, nc.vector.tensor_copy, None, head[:, 4 * HALF : 6 * HALF])
 
-        def quantise_g(h, grouped):
-            interleave(nc.vector.tensor_copy, grouped, g_raw[h][:])
-            cols = slice((h + 1) * HALF, (h + 2) * HALF)
+        def quantise_g(first, grouped):
+            cols = slice(HALF + first, HALF + first + grouped.shape[1] // LANES)
             nc.vector.quantize_mx(out=g_codes[:, cols].bitcast(E5M2), scales=g_scales[:, cols], in_=grouped)
 
-        quantise_g(0, head[:, : LANES * HALF])
+        for c in range(2):
+            interleave(nc.vector.tensor_copy, head[:, 2 * c * HALF : 2 * (c + 1) * HALF], g_raw[c][:])
+            quantise_g(c * QUARTER, head[:, 2 * c * HALF : 2 * (c + 1) * HALF])
         early = product("early", x_quant, (g_codes[:, :SLOTS], g_scales[:, :SLOTS]), "bank_early")
-        quantise_g(1, head[:, K:])
+        interleave(nc.vector.tensor_copy, head[:, 3 * HALF : 5 * HALF], g_raw[2][:, :, :QUARTER])
+        interleave(nc.scalar.copy, head[:, 5 * HALF :], g_raw[2][:, :, QUARTER:])
+        quantise_g(HALF, head[:, 3 * HALF :])
         g_quant = (g_codes[:, HALF:], g_scales[:, HALF:])
 
         def quantise_v(h, tag):
@@ -186,33 +192,29 @@ def tile_attend_gtied_pl_kernel(tc, V, dz, xT, G, offs, joffs, out_0, out_1, out
                 round_pair(nc.scalar.copy, 0, slice(0, TOKENS))
 
         quarter = TOKENS // 4
-        half = TOKENS // 2
-        for q in range(4):
-            cols = slice(q * quarter, (q + 1) * quarter)
+        split = 640
+        for cols in (slice(0, quarter), slice(split, TOKENS), slice(quarter, split)):
             nc.vector.tensor_tensor(total[:, cols], pa[1][:, cols], pb[3][:, cols], ADD)
-            if q < 2:
-                round_pair(nc.scalar.copy, 1, cols)
-            if q % 2 == 1:
-                cols = slice((q // 2) * half, (q // 2 + 1) * half)
-                nc.sync.dma_start(out=out_rows[:, 3, cols], in_=total[:, cols])
-        for q in range(2, 4):
-            round_pair(nc.vector.tensor_copy, 1, slice(q * quarter, (q + 1) * quarter))
+            nc.sync.dma_start(out=out_rows[:, 3, cols], in_=total[:, cols])
+        for cols in (slice(0, quarter), slice(quarter, 2 * quarter), slice(2 * quarter, split)):
+            round_pair(nc.scalar.copy, 1, cols)
+        round_pair(nc.vector.tensor_copy, 1, slice(split, TOKENS))
 
         words = tile("words", [P, TOKENS], U32)
-        scales = tile("scales", [P, TOKENS], U8)
+        scales = tile("scales", [P, quarter], U8)
         words_out = out_1.rearrange("a p c j -> p (a c j)").bitcast(I32)
-        for first, last in ((0, half), (half, half + quarter), (half + quarter, TOKENS)):
-            cols = slice(first, last)
+        for q in (0, 3, 1, 2):
+            cols = slice(q * quarter, (q + 1) * quarter)
             nc.vector.quantize_mx(
                 out=words[:, cols].bitcast(E4M3),
-                scales=scales[:, cols],
-                in_=rounded[:, first * LANES : last * LANES],
+                scales=scales[4 * q :, :],
+                in_=rounded[:, q * quarter * LANES : (q + 1) * quarter * LANES],
             )
             nc.sync.dma_start(out=words_out[:, cols], in_=words[:, cols].bitcast(I32))
         scales_out = out_2.rearrange("a b c -> (a b) c").bitcast(I32)
         for quadrant in range(4):
             queue = nc.scalar if quadrant % 2 == 0 else nc.sync
             queue.dma_start(
-                out=scales_out[4 * quadrant : 4 * quadrant + 4, :],
-                in_=scales[32 * quadrant : 32 * quadrant + 4, :].bitcast(I32),
+                out=scales_out[4 * quadrant : 4 * quadrant + 4, :].rearrange("r (q c) -> q r c", q=4),
+                in_=scales[32 * quadrant : 32 * quadrant + 16, :].bitcast(I32),
             )

@@ -18,8 +18,11 @@ LANES = 4
 K = P * LANES
 SLOTS = 512
 HALF = SLOTS // 2
-QUARTER = SLOTS // 4
+BAND = 16
 TOKENS = 1024
+QUARTER = TOKENS // 4
+FIRST_PART = 192
+SPLIT = 640
 
 FLOPS = 2 * 2 * K * K * SLOTS
 
@@ -37,12 +40,10 @@ def tile_attend_gtied_pl_kernel(tc, V, dz, xT, G, offs, joffs, out_0, out_1, out
         x_raw = [tile("x_raw%d" % t, [P, K], F32) for t in range(LANES)]
         nc.sync.dma_start(out=x_raw[0][:], in_=x_rows[:, 0, :])
         g_rows = G.rearrange("(p j) i -> p j i", j=LANES)
-        g_raw = []
-        for first, last in ((0, QUARTER), (QUARTER, HALF), (HALF, SLOTS)):
-            raw = tile("g_raw%d" % first, [P, LANES, last - first], F32)
-            nc.sync.dma_start(out=raw[:], in_=g_rows[:, :, first:last])
-            g_raw.append(raw)
-        idx = sb.tile([P, SLOTS // 16], U16, name="idx")
+        g_raw = [tile("g_raw%d" % h, [P, LANES, HALF], F32) for h in range(2)]
+        for h in range(2):
+            nc.sync.dma_start(out=g_raw[h][:], in_=g_rows[:, :, h * HALF : (h + 1) * HALF])
+        idx = sb.tile([P, SLOTS // BAND], U16, name="idx")
         nc.sync.dma_start(idx[:], offs)
         for t in (1, 2):
             nc.sync.dma_start(out=x_raw[t][:], in_=x_rows[:, t, :])
@@ -51,7 +52,7 @@ def tile_attend_gtied_pl_kernel(tc, V, dz, xT, G, offs, joffs, out_0, out_1, out
         nc.sync.dma_start(out=x_raw[3][:], in_=x_rows[:, 3, :])
         dz_raw = tile("dz_raw", [P, LANES, SLOTS], F32)
         nc.sync.dma_start(out=dz_raw[:], in_=dz.rearrange("(p j) s -> p j s", j=LANES))
-        jdx = sb.tile([P, SLOTS // 16], U16, name="jdx")
+        jdx = sb.tile([P, SLOTS // BAND], U16, name="jdx")
         nc.sync.dma_start(jdx[:], joffs)
 
         ident = tile("ident", [P, P], F32)
@@ -66,7 +67,7 @@ def tile_attend_gtied_pl_kernel(tc, V, dz, xT, G, offs, joffs, out_0, out_1, out
         g_scales = tile("g_scales", [P, HALF + SLOTS], U8)
         nc.vector.memset(g_codes[:, 0:HALF], 0)
         nc.vector.memset(g_scales[:, 0:HALF].bitcast(U32), 0)
-        pb = [window("pb0", nc.vector), window("pb1", nc.gpsimd)]
+        pb = [window("pb0", nc.vector), window("pb1", nc.vector)]
 
         def interleave(copy, grouped, raw):
             copy(
@@ -87,10 +88,10 @@ def tile_attend_gtied_pl_kernel(tc, V, dz, xT, G, offs, joffs, out_0, out_1, out
                 out=pairs[:].rearrange("m (u p e) -> m u p e", u=2, e=2),
                 in_=x_raw[t][:].rearrange("m (p u e) -> m u p e", u=2, e=2),
             )
-            words = pairs[:].bitcast(F32)
+            pair_words = pairs[:].bitcast(F32)
             turned = ps.tile([P, 2, P], F32, name="turned%d" % t, tag="turned")
             for u in range(2):
-                nc.tensor.transpose(turned[:, u, :], words[:, u * P : (u + 1) * P], ident[:])
+                nc.tensor.transpose(turned[:, u, :], pair_words[:, u * P : (u + 1) * P], ident[:])
             nc.scalar.copy(
                 out=grouped.bitcast(F32).rearrange("p (m u) -> p m u", u=2),
                 in_=turned[:].rearrange("p u m -> p m u"),
@@ -114,24 +115,20 @@ def tile_attend_gtied_pl_kernel(tc, V, dz, xT, G, offs, joffs, out_0, out_1, out
             count = results.shape[1]
             staged = tile(name, [P, count], F32, tag=tag)
             nc.scalar.copy(out=staged[:], in_=results)
-            entries = offsets[:, first // 16 : (first + count) // 16]
+            entries = offsets[:, first // BAND : (first + count) // BAND]
             nc.vector.tensor_copy(target[:].indirect(entries), staged[:])
-            return staged
 
-        head = tile("head", [P, 7 * HALF], BF16)
-        x_quant = quantise_x(0, nc.vector.tensor_copy, None, head[:, 4 * HALF : 6 * HALF])
+        head = tile("head", [P, LANES * HALF + K], BF16)
+        x_quant = quantise_x(0, nc.vector.tensor_copy, None, head[:, LANES * HALF :])
 
-        def quantise_g(first, grouped):
-            cols = slice(HALF + first, HALF + first + grouped.shape[1] // LANES)
+        def quantise_g(h, grouped):
+            interleave(nc.vector.tensor_copy, grouped, g_raw[h][:])
+            cols = slice((h + 1) * HALF, (h + 2) * HALF)
             nc.vector.quantize_mx(out=g_codes[:, cols].bitcast(E5M2), scales=g_scales[:, cols], in_=grouped)
 
-        for c in range(2):
-            interleave(nc.vector.tensor_copy, head[:, 2 * c * HALF : 2 * (c + 1) * HALF], g_raw[c][:])
-            quantise_g(c * QUARTER, head[:, 2 * c * HALF : 2 * (c + 1) * HALF])
+        quantise_g(0, head[:, : LANES * HALF])
         early = product("early", x_quant, (g_codes[:, :SLOTS], g_scales[:, :SLOTS]), "bank_early")
-        interleave(nc.vector.tensor_copy, head[:, 3 * HALF : 5 * HALF], g_raw[2][:, :, :QUARTER])
-        interleave(nc.scalar.copy, head[:, 5 * HALF :], g_raw[2][:, :, QUARTER:])
-        quantise_g(HALF, head[:, 3 * HALF :])
+        quantise_g(1, head[:, K:])
         g_quant = (g_codes[:, HALF:], g_scales[:, HALF:])
 
         def quantise_v(h, tag):
@@ -145,12 +142,13 @@ def tile_attend_gtied_pl_kernel(tc, V, dz, xT, G, offs, joffs, out_0, out_1, out
         freed = "head"
         for t in range(LANES - 1):
             db = product("db%d" % t, x_quant, g_quant, "bank_db%d" % (t % 2))
-            staged = scatter("db%da" % t, pb[t], idx, 0, early[:, HALF:] if t == 0 else db[:, :HALF])
+            cut = HALF if t == 0 else FIRST_PART
+            scatter("db%da" % t, pb[t], idx, 0, early[:, HALF:] if t == 0 else db[:, :cut])
             grouped = tile("x_grouped%d" % (t + 1), [P, K], BF16)
             x_quant = quantise_x(t + 1, nc.scalar.copy, freed, grouped[:])
-            scatter("db%db" % t, pb[t], idx, HALF, db[:, HALF:], tag=freed)
+            scatter("db%db" % t, pb[t], idx, cut, db[:, cut:], tag=freed)
             freed = "x_grouped%d" % (t + 1)
-            if t < 2:
+            if t + 2 < LANES:
                 pb.append(window("pb%d" % (t + 2), nc.gpsimd, tag="x%d_scales" % t))
             if t == 1:
                 v_quant = [quantise_v(0, "x1_codes")]
@@ -191,24 +189,22 @@ def tile_attend_gtied_pl_kernel(tc, V, dz, xT, G, offs, joffs, out_0, out_1, out
             if t == 1:
                 round_pair(nc.scalar.copy, 0, slice(0, TOKENS))
 
-        quarter = TOKENS // 4
-        split = 640
-        for cols in (slice(0, quarter), slice(split, TOKENS), slice(quarter, split)):
+        for cols in (slice(0, QUARTER), slice(SPLIT, TOKENS), slice(QUARTER, SPLIT)):
             nc.vector.tensor_tensor(total[:, cols], pa[1][:, cols], pb[3][:, cols], ADD)
             nc.sync.dma_start(out=out_rows[:, 3, cols], in_=total[:, cols])
-        for cols in (slice(0, quarter), slice(quarter, 2 * quarter), slice(2 * quarter, split)):
+        for cols in (slice(0, QUARTER), slice(QUARTER, 2 * QUARTER), slice(2 * QUARTER, SPLIT)):
             round_pair(nc.scalar.copy, 1, cols)
-        round_pair(nc.vector.tensor_copy, 1, slice(split, TOKENS))
+        round_pair(nc.vector.tensor_copy, 1, slice(SPLIT, TOKENS))
 
         words = tile("words", [P, TOKENS], U32)
-        scales = tile("scales", [P, quarter], U8)
+        scales = tile("scales", [P, QUARTER], U8)
         words_out = out_1.rearrange("a p c j -> p (a c j)").bitcast(I32)
         for q in (0, 3, 1, 2):
-            cols = slice(q * quarter, (q + 1) * quarter)
+            cols = slice(q * QUARTER, (q + 1) * QUARTER)
             nc.vector.quantize_mx(
                 out=words[:, cols].bitcast(E4M3),
                 scales=scales[4 * q :, :],
-                in_=rounded[:, q * quarter * LANES : (q + 1) * quarter * LANES],
+                in_=rounded[:, q * QUARTER * LANES : (q + 1) * QUARTER * LANES],
             )
             nc.sync.dma_start(out=words_out[:, cols], in_=words[:, cols].bitcast(I32))
         scales_out = out_2.rearrange("a b c -> (a b) c").bitcast(I32)

from contextlib import ExitStack

import concourse.mybir as mybir
from concourse.masks import make_identity

F32 = mybir.dt.float32
BF16 = mybir.dt.bfloat16
I32 = mybir.dt.int32
U32 = mybir.dt.uint32
U16 = mybir.dt.uint16
U8 = mybir.dt.uint8
E4M3 = mybir.dt.float8_e4m3fn_x4
E5M2 = mybir.dt.float8_e5m2_x4
ADD = mybir.AluOpType.add

P = 128
LANES = 4
K = P * LANES
SLOTS = 512
HALF = SLOTS // 2
BAND = 16
TOKENS = 1024
QUARTER = TOKENS // 4
FIRST_PART = 192
SPLIT = 640

FLOPS = 2 * 2 * K * K * SLOTS


def tile_attend_gtied_pl_kernel(tc, V, dz, xT, G, offs, joffs, out_0, out_1, out_2):
    nc = tc.nc
    with ExitStack() as ctx:
        sb = ctx.enter_context(tc.tile_pool(name="sb", bufs=1))
        ps = ctx.enter_context(tc.psum_pool(name="ps", bufs=1))

        def tile(name, shape, dtype, tag=None):
            return sb.tile(shape, dtype, name=name, tag=tag or name, align_bytes=64)

        x_rows = xT.rearrange("(m t) r -> m t r", t=LANES)
        x_raw = [tile("x_raw%d" % t, [P, K], F32) for t in range(LANES)]
        nc.sync.dma_start(out=x_raw[0][:], in_=x_rows[:, 0, :])
        g_rows = G.rearrange("(p j) i -> p j i", j=LANES)
        g_raw = [tile("g_raw%d" % h, [P, LANES, HALF], F32) for h in range(2)]
        for h in range(2):
            nc.sync.dma_start(out=g_raw[h][:], in_=g_rows[:, :, h * HALF : (h + 1) * HALF])
        idx = sb.tile([P, SLOTS // BAND], U16, name="idx")
        nc.sync.dma_start(idx[:], offs)
        for t in (1, 2):
            nc.sync.dma_start(out=x_raw[t][:], in_=x_rows[:, t, :])
        v_raw = tile("v_raw", [P, LANES, K], F32)
        nc.sync.dma_start(out=v_raw[:], in_=V.rearrange("(p j) d -> p j d", j=LANES))
        nc.sync.dma_start(out=x_raw[3][:], in_=x_rows[:, 3, :])
        dz_raw = tile("dz_raw", [P, LANES, SLOTS], F32)
        nc.sync.dma_start(out=dz_raw[:], in_=dz.rearrange("(p j) s -> p j s", j=LANES))
        jdx = sb.tile([P, SLOTS // BAND], U16, name="jdx")
        nc.sync.dma_start(jdx[:], joffs)

        ident = tile("ident", [P, P], F32)
        make_identity(nc, ident[:])

        def window(name, engine, tag=None):
            cleared = tile(name, [P, TOKENS], F32, tag=tag)
            engine.memset(cleared[:].bitcast(I32), 0)
            return cleared

        g_codes = tile("g_codes", [P, HALF + SLOTS], U32)
        g_scales = tile("g_scales", [P, HALF + SLOTS], U8)
        nc.vector.memset(g_codes[:, 0:HALF], 0)
        nc.vector.memset(g_scales[:, 0:HALF].bitcast(U32), 0)
        pb = [window("pb0", nc.vector), window("pb1", nc.vector)]

        def interleave(copy, grouped, raw):
            copy(
                out=grouped.rearrange("p (c i j) -> p c j i", i=4, j=LANES),
                in_=raw.rearrange("p j (c i) -> p c j i", i=4),
            )

        def quantise(name, grouped, fmt):
            width = grouped.shape[1] // LANES
            codes = tile(name + "_codes", [P, width], U32)
            scales = tile(name + "_scales", [P, width], U8)
            nc.vector.quantize_mx(out=codes[:].bitcast(fmt), scales=scales[:], in_=grouped)
            return codes[:], scales[:]

        def quantise_x(t, cast, pairs_tag, grouped):
            pairs = tile("x_pairs%d" % t, [P, K], BF16, tag=pairs_tag)
            cast(
                out=pairs[:].rearrange("m (u p e) -> m u p e", u=2, e=2),
                in_=x_raw[t][:].rearrange("m (p u e) -> m u p e", u=2, e=2),
            )
            pair_words = pairs[:].bitcast(F32)
            turned = ps.tile([P, 2, P], F32, name="turned%d" % t, tag="turned")
            for u in range(2):
                nc.tensor.transpose(turned[:, u, :], pair_words[:, u * P : (u + 1) * P], ident[:])
            nc.scalar.copy(
                out=grouped.bitcast(F32).rearrange("p (m u) -> p m u", u=2),
                in_=turned[:].rearrange("p u m -> p m u"),
            )
            return quantise("x%d" % t, grouped, E4M3)

        def product(name, stationary, moving, bank_tag):
            bank = ps.tile([P, SLOTS], F32, name="bank_" + name, tag=bank_tag)
            nc.tensor.matmul_mx(
                out=bank[:],
                lhsT=stationary[0].bitcast(E4M3),
                lhsT_scale=stationary[1],
                rhs=moving[0].bitcast(E5M2),
                rhs_scale=moving[1],
                start=True,
                stop=True,
            )
            return bank

        def scatter(name, target, offsets, first, results, tag=None):
            count = results.shape[1]
            staged = tile(name, [P, count], F32, tag=tag)
            nc.scalar.copy(out=staged[:], in_=results)
            entries = offsets[:, first // BAND : (first + count) // BAND]
            nc.vector.tensor_copy(target[:].indirect(entries), staged[:])

        head = tile("head", [P, LANES * HALF + K], BF16)
        x_quant = quantise_x(0, nc.vector.tensor_copy, None, head[:, LANES * HALF :])

        def quantise_g(h, grouped):
            interleave(nc.vector.tensor_copy, grouped, g_raw[h][:])
            cols = slice((h + 1) * HALF, (h + 2) * HALF)
            nc.vector.quantize_mx(out=g_codes[:, cols].bitcast(E5M2), scales=g_scales[:, cols], in_=grouped)

        quantise_g(0, head[:, : LANES * HALF])
        early = product("early", x_quant, (g_codes[:, :SLOTS], g_scales[:, :SLOTS]), "bank_early")
        quantise_g(1, head[:, K:])
        g_quant = (g_codes[:, HALF:], g_scales[:, HALF:])

        def quantise_v(h, tag):
            grouped = tile("v_grouped%d" % h, [P, 2 * K], BF16, tag=tag)
            nc.scalar.copy(
                out=grouped[:].rearrange("p (t m j) -> p m t j", t=2, j=LANES),
                in_=v_raw[:].rearrange("p j (m t) -> p m t j", t=LANES)[:, :, 2 * h : 2 * h + 2, :],
            )
            return quantise("v%d" % h, grouped[:], E4M3)

        freed = "head"
        for t in range(LANES - 1):
            db = product("db%d" % t, x_quant, g_quant, "bank_db%d" % (t % 2))
            cut = HALF if t == 0 else FIRST_PART
            scatter("db%da" % t, pb[t], idx, 0, early[:, HALF:] if t == 0 else db[:, :cut])
            grouped = tile("x_grouped%d" % (t + 1), [P, K], BF16)
            x_quant = quantise_x(t + 1, nc.scalar.copy, freed, grouped[:])
            scatter("db%db" % t, pb[t], idx, cut, db[:, cut:], tag=freed)
            freed = "x_grouped%d" % (t + 1)
            if t + 2 < LANES:
                pb.append(window("pb%d" % (t + 2), nc.gpsimd, tag="x%d_scales" % t))
            if t == 1:
                v_quant = [quantise_v(0, "x1_codes")]

        dz_grouped = tile("dz_grouped", [P, LANES * SLOTS], BF16, tag="x2_codes")
        for h in range(2):
            interleave(
                nc.scalar.copy,
                dz_grouped[:, h * LANES * HALF : (h + 1) * LANES * HALF],
                dz_raw[:, :, h * HALF : (h + 1) * HALF],
            )
        dz_quant = quantise("dz", dz_grouped[:], E5M2)
        db = product("db3", x_quant, g_quant, "bank_db1")
        scatter("db3", pb[3], idx, 0, db[:], tag="dz_raw")
        v_quant.append(quantise_v(1, "x3_codes"))
        pa = [window("pa0", nc.gpsimd, tag="x3_scales"), window("pa1", nc.gpsimd, tag="x2_codes")]

        out_rows = out_0.rearrange("(p t) c -> p t c", t=LANES)
        sums = [tile("sums%d" % h, [P, 2 * TOKENS], F32) for h in range(2)]
        rounded = tile("rounded", [P, LANES * TOKENS], BF16)
        rounded_cols = rounded[:].rearrange("p (c j) -> p c j", j=LANES)

        def round_pair(copy, h, cols):
            copy(
                out=rounded_cols[:, cols, 2 * h : 2 * h + 2],
                in_=sums[h][:].rearrange("p (e c) -> p c e", e=2)[:, cols, :],
            )

        for t in range(LANES):
            cols = slice((t % 2) * P, (t % 2 + 1) * P)
            v_codes, v_scales = v_quant[t // 2]
            da = product("da%d" % t, (v_codes[:, cols], v_scales[:, cols]), dz_quant, "bank_da%d" % t)
            scatter("da%d" % t, pa[t % 2], jdx, 0, da[:])
            total = sums[t // 2][:, (t % 2) * TOKENS : (t % 2 + 1) * TOKENS]
            if t < LANES - 1:
                nc.gpsimd.tensor_tensor(total, pa[t % 2][:], pb[t][:], ADD)
                nc.sync.dma_start(out=out_rows[:, t, :], in_=total)
            if t == 1:
                round_pair(nc.scalar.copy, 0, slice(0, TOKENS))

        for cols in (slice(0, QUARTER), slice(SPLIT, TOKENS), slice(QUARTER, SPLIT)):
            nc.vector.tensor_tensor(total[:, cols], pa[1][:, cols], pb[3][:, cols], ADD)
            nc.sync.dma_start(out=out_rows[:, 3, cols], in_=total[:, cols])
        for cols in (slice(0, QUARTER), slice(QUARTER, 2 * QUARTER), slice(2 * QUARTER, SPLIT)):
            round_pair(nc.scalar.copy, 1, cols)
        round_pair(nc.vector.tensor_copy, 1, slice(SPLIT, TOKENS))

        words = tile("words", [P, TOKENS], U32)
        scales = tile("scales", [P, QUARTER], U8)
        words_out = out_1.rearrange("a p c j -> p (a c j)").bitcast(I32)
        for q in (0, 3, 1, 2):
            cols = slice(q * QUARTER, (q + 1) * QUARTER)
            nc.vector.quantize_mx(
                out=words[:, cols].bitcast(E4M3),
                scales=scales[4 * q :, :],
                in_=rounded[:, q * QUARTER * LANES : (q + 1) * QUARTER * LANES],
            )
            nc.sync.dma_start(out=words_out[:, cols], in_=words[:, cols].bitcast(I32))
        scales_out = out_2.rearrange("a b c -> (a b) c").bitcast(I32)
        for quadrant in range(4):
            queue = nc.scalar if quadrant % 2 == 0 else nc.sync
            queue.dma_start(
                out=scales_out[4 * quadrant : 4 * quadrant + 4, :].rearrange("r (q c) -> q r c", q=4),
                in_=scales[32 * quadrant : 32 * quadrant + 16, :].bitcast(I32),
            )
